import numpy as np
import ml_dtypes


def mxq(x, axis, fmt="e4m3"):
    dtype, down = {"e4m3": (ml_dtypes.float8_e4m3fn, 7), "e5m2": (ml_dtypes.float8_e5m2, 14)}[fmt]
    v = np.moveaxis(np.asarray(x, np.float32).astype(ml_dtypes.bfloat16).astype(np.float64), axis, -1)
    blocks = v.reshape(v.shape[:-1] + (-1, 32))
    amax = np.abs(blocks).max(-1, keepdims=True)
    byte = np.maximum(np.where(amax > 0, np.frexp(amax)[1] - 1 + 127, 0) - down, 1)
    scale = np.exp2(byte - 127.0)
    codes = (blocks / scale).astype(np.float32).astype(dtype).astype(np.float64)
    return np.moveaxis((codes * scale).reshape(v.shape), -1, axis)


WIDE = False


def mx_kscale(k):
    if not WIDE:
        return np.ones(k)
    levels = np.array([10, -10, 5, -5, 0])
    if k % 512:
        return np.exp2(np.random.permutation(np.resize(levels, k // 32))).repeat(32)
    a = np.empty((k // 512, 16))
    for p in range(k // 512):
        a[p, :8] = np.random.permutation(np.resize(levels, 8))
        for g in range(8):
            far = levels[np.abs(levels - a[p, g]) >= 10]
            a[p, g + 8] = far[np.random.randint(len(far))]
    return np.exp2(a.ravel()).repeat(32)


def f64(x):
    return np.asarray(x).astype(np.float64)


def striped(idx):
    return np.tile(idx.reshape(-1, 16).T, (8, 1)).astype(np.uint16)


def unstriped(offs):
    return offs[:16].T.reshape(-1).astype(np.int64)


def pack_weight(w):
    k, n = w.shape
    w = f64(np.asarray(w, np.float32).astype(ml_dtypes.bfloat16)).reshape(k // 32, 32, n)
    amax = np.abs(w).max(1)
    byte = np.clip(np.where(amax > 0, np.frexp(amax)[1] - 1 + 127 - 7, 1), 1, 254)
    scaled = (w * np.exp2(127.0 - byte)[:, None, :]).reshape(k, n).astype(np.float32)
    words = np.ascontiguousarray(scaled.reshape(k // 512, 128, 4, n).transpose(0, 1, 3, 2)).astype(ml_dtypes.float8_e4m3fn).view(np.uint8)
    return words, np.ascontiguousarray(byte.astype(np.uint8).reshape(k // 512, 16, n))


def unpack_weight(words, scales):
    g, p, n, _ = words.shape
    vals = np.ascontiguousarray(words).view(ml_dtypes.float8_e4m3fn).astype(np.float64) * np.repeat(np.exp2(scales.astype(np.float64) - 127.0), 8, axis=1)[..., None]
    return vals.transpose(0, 1, 3, 2).reshape(g * 512, n)


K, T, S, V, N = 512, 4096, 1024, 512, 128


def setup_inputs():
    n = np.random.standard_normal
    s = mx_kscale(K)[:, None]
    packed_xT = pack_weight(n((K, T)) * s)
    return {
        "x_words": packed_xT[0],
        "x_scales": packed_xT[1],
        "sT": (n((K, V)) * s).astype(np.float32),
        "w1": (n((K, N)) / np.sqrt(K) / s).astype(np.float32),
        "w2": (n((K, N)) / np.sqrt(K) / s).astype(np.float32),
        "offs": striped(np.random.permutation(T)[:S]),
        "par": striped(np.random.randint(0, V, S)),
    }


def reference(x_words, x_scales, sT, w1, w2, offs, par):
    xq = unpack_weight(x_words, x_scales)[:, unstriped(offs)]
    y = mxq(f64(w1), 0, "e4m3").T @ xq
    t = mxq(f64(w2), 0, "e4m3").T @ mxq(f64(sT), 0, "e4m3")
    return y + t[:, unstriped(par)]

@@ -1,0 +1,119 @@
+from contextlib import ExitStack
+
+import concourse.mybir as mybir
+
+K, T, S, V, N = 512, 4096, 1024, 512, 128
+FLOPS = 2 * K * N * (S + V)
+
+F32 = mybir.dt.float32
+BF16 = mybir.dt.bfloat16
+I32 = mybir.dt.int32
+U32 = mybir.dt.uint32
+U16 = mybir.dt.uint16
+U8 = mybir.dt.uint8
+FP8X4 = mybir.dt.float8_e4m3fn_x4
+ADD = mybir.AluOpType.add
+
+P = 128
+PACK = 4
+LIST_ROWS = 16
+
+
+def interleave(copy, grouped, raw):
+    copy(
+        out=grouped.rearrange("p (c i t) -> p c t i", i=4, t=PACK),
+        in_=raw.rearrange("p t (c i) -> p c t i", i=4),
+    )
+
+
+def tile_picked_fpn_none_p_kernel(
+    tc, x_words, x_scales, sT, w1, w2, offs, par, out
+):
+    nc = tc.nc
+    with ExitStack() as ctx:
+        pool = ctx.enter_context(tc.tile_pool(name="sbuf", bufs=1))
+        psum = ctx.enter_context(tc.psum_pool(name="psum", bufs=1))
+
+        offs_sb = pool.tile([P, S // LIST_ROWS], U16, name="offs_sb")
+        par_sb = pool.tile([P, S // LIST_ROWS], U16, name="par_sb")
+        word_table = pool.tile([P, T], I32, name="word_table", align_bytes=64)
+        scale_table = pool.tile([P, T], U8, name="scale_table", align_bytes=64)
+        scale_picked = pool.tile([P, S], U8, name="scale_picked", align_bytes=64)
+        x_plane = pool.tile([P, S], U8, name="x_plane", align_bytes=64)
+        w1_raw = pool.tile([P, PACK, N], F32, name="w1_raw", align_bytes=64)
+        w2_raw = pool.tile([P, PACK, N], F32, name="w2_raw", align_bytes=64)
+        s_raw = [pool.tile([P, PACK, V // 2], F32, name=f"s_raw{h}", align_bytes=64) for h in range(2)]
+
+        nc.vector.memset(scale_table[0:112, :].bitcast(I32), 0)
+        nc.vector.memset(x_plane[:].bitcast(I32), 0)
+
+        nc.sync.dma_start(scale_table[112:P, :].bitcast(I32), x_scales[0].bitcast(I32))
+        nc.sync.dma_start(offs_sb[:], offs)
+        nc.sync.dma_start(w2_raw[:], w2.rearrange("(p j) m -> p j m", j=PACK))
+        s_rows = sT.rearrange("(p j) v -> p j v", j=PACK)
+        for h in range(2):
+            nc.sync.dma_start(s_raw[h][:], s_rows[:, :, h * (V // 2) : (h + 1) * (V // 2)])
+        nc.sync.dma_start(w1_raw[:], w1.rearrange("(p j) m -> p j m", j=PACK))
+        nc.sync.dma_start(par_sb[:], par)
+        nc.sync.dma_start(word_table[:], x_words[0].rearrange("p c r -> p (c r)").bitcast(I32))
+
+        nc.vector.tensor_copy(scale_picked[:], scale_table[:].indirect(offs_sb[:]))
+
+        def quantize(name, raw, copy):
+            width = raw.shape[2]
+            grouped = pool.tile([P, PACK * width], BF16, name=f"{name}_grouped", align_bytes=64)
+            codes = pool.tile([P, width], U32, name=f"{name}_codes", align_bytes=64)
+            plane = pool.tile([P, width], U8, name=f"{name}_plane", align_bytes=64)
+            interleave(copy, grouped[:], raw)
+            nc.vector.quantize_mx(out=codes[:].bitcast(FP8X4), scales=plane[:], in_=grouped[:])
+            return codes, plane
+
+        w2_codes, w2_plane = quantize("w2", w2_raw[:], nc.scalar.copy)
+        coarse = pool.tile([P, V], F32, name="coarse", align_bytes=64)
+        pieces = [
+            (0, s_raw[0][:], nc.scalar.copy),
+            (256, s_raw[1][:, :, 0:128], nc.scalar.copy),
+            (384, s_raw[1][:, :, 128:256], nc.vector.tensor_copy),
+        ]
+        for v0, raw, copy in pieces:
+            width = raw.shape[2]
+            codes, plane = quantize(f"s{v0}", raw, copy)
+            acc = psum.tile([P, width], F32, name=f"coarse_acc{v0}")
+            nc.tensor.matmul_mx(
+                out=acc[:], lhsT=w2_codes[:].bitcast(FP8X4), lhsT_scale=w2_plane[:],
+                rhs=codes[:].bitcast(FP8X4), rhs_scale=plane[:], start=True, stop=True,
+            )
+            nc.scalar.copy(out=coarse[:, v0 : v0 + width], in_=acc[:])
+
+        w1_codes, w1_plane = quantize("w1", w1_raw[:], nc.scalar.copy)
+
+        for r in range(4):
+            nc.sync.dma_start(
+                x_plane[r:P:32, :].bitcast(I32), scale_picked[112 + r : P : 4, :].bitcast(I32)
+            )
+
+        parents = pool.tile([P, S], F32, name="parents", align_bytes=64)
+        for q in range(4):
+            nc.vector.tensor_copy(
+                parents[:, 256 * q : 256 * (q + 1)],
+                coarse[:].indirect(par_sb[:, 16 * q : 16 * (q + 1)]),
+            )
+
+        picked = [pool.tile([P, S // 2], U32, name=f"picked{h}", align_bytes=64) for h in range(2)]
+        for h in range(2):
+            nc.vector.tensor_copy(
+                picked[h][:], word_table[:].bitcast(U32).indirect(offs_sb[:, 32 * h : 32 * (h + 1)])
+            )
+        for j0, width, step in ((0, 512, 512), (512, 256, 128), (768, 256, 128)):
+            result = pool.tile([P, width], F32, name=f"result{j0}", align_bytes=64)
+            for j in range(j0, j0 + width, step):
+                cols = slice(j, j + step)
+                c0 = j % 512
+                acc = psum.tile([P, step], F32, name=f"fine_acc{j}")
+                nc.tensor.matmul_mx(
+                    out=acc[:], lhsT=w1_codes[:].bitcast(FP8X4), lhsT_scale=w1_plane[:],
+                    rhs=picked[j // 512][:, c0 : c0 + step].bitcast(FP8X4), rhs_scale=x_plane[:, cols],
+                    start=True, stop=True,
+                )
+                nc.vector.tensor_tensor(result[:, j - j0 : j - j0 + step], acc[:], parents[:, cols], ADD)
+            nc.sync.dma_start(out[:, j0 : j0 + width], result[:])

@@ -42,7 +42,7 @@ def tile_picked_fpn_none_p_kernel(
         x_plane = pool.tile([P, S], U8, name="x_plane", align_bytes=64)
         w1_raw = pool.tile([P, PACK, N], F32, name="w1_raw", align_bytes=64)
         w2_raw = pool.tile([P, PACK, N], F32, name="w2_raw", align_bytes=64)
-        s_raw = [pool.tile([P, PACK, V // 2], F32, name=f"s_raw{h}", align_bytes=64) for h in range(2)]
+        s_raw = pool.tile([P, PACK, V], F32, name="s_raw", align_bytes=64)
 
         nc.vector.memset(scale_table[0:112, :].bitcast(I32), 0)
         nc.vector.memset(x_plane[:].bitcast(I32), 0)
@@ -50,42 +50,40 @@ def tile_picked_fpn_none_p_kernel(
         nc.sync.dma_start(scale_table[112:P, :].bitcast(I32), x_scales[0].bitcast(I32))
         nc.sync.dma_start(offs_sb[:], offs)
         nc.sync.dma_start(w2_raw[:], w2.rearrange("(p j) m -> p j m", j=PACK))
-        s_rows = sT.rearrange("(p j) v -> p j v", j=PACK)
-        for h in range(2):
-            nc.sync.dma_start(s_raw[h][:], s_rows[:, :, h * (V // 2) : (h + 1) * (V // 2)])
+        nc.sync.dma_start(s_raw[:], sT.rearrange("(p j) v -> p j v", j=PACK))
         nc.sync.dma_start(w1_raw[:], w1.rearrange("(p j) m -> p j m", j=PACK))
         nc.sync.dma_start(par_sb[:], par)
         nc.sync.dma_start(word_table[:], x_words[0].rearrange("p c r -> p (c r)").bitcast(I32))
 
         nc.vector.tensor_copy(scale_picked[:], scale_table[:].indirect(offs_sb[:]))
 
-        def quantize(name, raw, copy):
-            width = raw.shape[2]
-            grouped = pool.tile([P, PACK * width], BF16, name=f"{name}_grouped", align_bytes=64)
+        def group(name, raw, copy):
+            grouped = pool.tile([P, PACK * raw.shape[2]], BF16, name=f"{name}_grouped", align_bytes=64)
+            interleave(copy, grouped[:], raw)
+            return grouped
+
+        def quantize(name, grouped):
+            width = grouped.shape[1] // PACK
             codes = pool.tile([P, width], U32, name=f"{name}_codes", align_bytes=64)
             plane = pool.tile([P, width], U8, name=f"{name}_plane", align_bytes=64)
-            interleave(copy, grouped[:], raw)
             nc.vector.quantize_mx(out=codes[:].bitcast(FP8X4), scales=plane[:], in_=grouped[:])
             return codes, plane
 
-        w2_codes, w2_plane = quantize("w2", w2_raw[:], nc.scalar.copy)
-        coarse = pool.tile([P, V], F32, name="coarse", align_bytes=64)
-        pieces = [
-            (0, s_raw[0][:], nc.scalar.copy),
-            (256, s_raw[1][:, :, 0:128], nc.scalar.copy),
-            (384, s_raw[1][:, :, 128:256], nc.vector.tensor_copy),
-        ]
-        for v0, raw, copy in pieces:
-            width = raw.shape[2]
-            codes, plane = quantize(f"s{v0}", raw, copy)
+        w2_codes, w2_plane = quantize("w2", group("w2", w2_raw[:], nc.scalar.copy))
+        coarse = pool.tile([P, V + 16], F32, name="coarse", align_bytes=64)
+        nc.vector.memset(coarse[:, V:], 0.0)
+        pieces = [(0, 128, nc.scalar.copy), (128, 256, nc.vector.tensor_copy), (384, 128, nc.scalar.copy)]
+        grouped = [group(f"s{v0}", s_raw[:, :, v0 : v0 + width], copy) for v0, width, copy in pieces]
+        for (v0, width, copy), values in zip(pieces, grouped):
+            codes, plane = quantize(f"s{v0}", values)
             acc = psum.tile([P, width], F32, name=f"coarse_acc{v0}")
             nc.tensor.matmul_mx(
                 out=acc[:], lhsT=w2_codes[:].bitcast(FP8X4), lhsT_scale=w2_plane[:],
                 rhs=codes[:].bitcast(FP8X4), rhs_scale=plane[:], start=True, stop=True,
             )
-            nc.scalar.copy(out=coarse[:, v0 : v0 + width], in_=acc[:])
+            copy(out=coarse[:, v0 : v0 + width], in_=acc[:])
 
-        w1_codes, w1_plane = quantize("w1", w1_raw[:], nc.scalar.copy)
+        w1_codes, w1_plane = quantize("w1", group("w1", w1_raw[:], nc.scalar.copy))
 
         for r in range(4):
             nc.sync.dma_start(
@@ -93,10 +91,10 @@ def tile_picked_fpn_none_p_kernel(
             )
 
         parents = pool.tile([P, S], F32, name="parents", align_bytes=64)
-        for q in range(4):
+        for q in range(2):
             nc.vector.tensor_copy(
-                parents[:, 256 * q : 256 * (q + 1)],
-                coarse[:].indirect(par_sb[:, 16 * q : 16 * (q + 1)]),
+                parents[:, 512 * q : 512 * (q + 1)],
+                coarse[:].indirect(par_sb[:, 32 * q : 32 * (q + 1)]),
             )
 
         picked = [pool.tile([P, S // 2], U32, name=f"picked{h}", align_bytes=64) for h in range(2)]

@@ -97,21 +97,26 @@ def tile_picked_fpn_none_p_kernel(
                 coarse[:].indirect(par_sb[:, 32 * q : 32 * (q + 1)]),
             )
 
+        results = [pool.tile([P, 256], F32, name=f"result{b}", align_bytes=64) for b in range(4)]
         picked = [pool.tile([P, S // 2], U32, name=f"picked{h}", align_bytes=64) for h in range(2)]
         for h in range(2):
             nc.vector.tensor_copy(
                 picked[h][:], word_table[:].bitcast(U32).indirect(offs_sb[:, 32 * h : 32 * (h + 1)])
             )
-        for j0, width, step in ((0, 512, 512), (512, 256, 128), (768, 256, 128)):
-            result = pool.tile([P, width], F32, name=f"result{j0}", align_bytes=64)
-            for j in range(j0, j0 + width, step):
-                cols = slice(j, j + step)
-                c0 = j % 512
-                acc = psum.tile([P, step], F32, name=f"fine_acc{j}")
-                nc.tensor.matmul_mx(
-                    out=acc[:], lhsT=w1_codes[:].bitcast(FP8X4), lhsT_scale=w1_plane[:],
-                    rhs=picked[j // 512][:, c0 : c0 + step].bitcast(FP8X4), rhs_scale=x_plane[:, cols],
-                    start=True, stop=True,
+        for j0, step in ((0, 512), (512, 128), (640, 128), (768, 128), (896, 128)):
+            acc = psum.tile([P, step], F32, name=f"fine_acc{j0}")
+            nc.tensor.matmul_mx(
+                out=acc[:], lhsT=w1_codes[:].bitcast(FP8X4), lhsT_scale=w1_plane[:],
+                rhs=picked[j0 // 512][:, j0 % 512 : j0 % 512 + step].bitcast(FP8X4),
+                rhs_scale=x_plane[:, j0 : j0 + step],
+                start=True, stop=True,
+            )
+            for j in range(j0, j0 + step, 256):
+                width = min(step, 256)
+                block = j // 256
+                nc.vector.tensor_tensor(
+                    results[block][:, j % 256 : j % 256 + width],
+                    acc[:, j - j0 : j - j0 + width], parents[:, j : j + width], ADD,
                 )
-                nc.vector.tensor_tensor(result[:, j - j0 : j - j0 + step], acc[:], parents[:, cols], ADD)
-            nc.sync.dma_start(out[:, j0 : j0 + width], result[:])
+                if (j + width) % 256 == 0:
+                    nc.sync.dma_start(out[:, 256 * block : 256 * (block + 1)], results[block][:])

@@ -51,14 +51,14 @@ def tile_picked_fpn_none_p_kernel(
         nc.sync.dma_start(offs_sb[:], offs)
         nc.sync.dma_start(w2_raw[:], w2.rearrange("(p j) m -> p j m", j=PACK))
         nc.sync.dma_start(s_raw[:], sT.rearrange("(p j) v -> p j v", j=PACK))
-        nc.sync.dma_start(w1_raw[:], w1.rearrange("(p j) m -> p j m", j=PACK))
         nc.sync.dma_start(par_sb[:], par)
         nc.sync.dma_start(word_table[:], x_words[0].rearrange("p c r -> p (c r)").bitcast(I32))
+        nc.sync.dma_start(w1_raw[:], w1.rearrange("(p j) m -> p j m", j=PACK))
 
         nc.vector.tensor_copy(scale_picked[:], scale_table[:].indirect(offs_sb[:]))
 
         def group(name, raw, copy):
-            grouped = pool.tile([P, PACK * raw.shape[2]], BF16, name=f"{name}_grouped", align_bytes=64)
+            grouped = pool.tile([P, PACK * raw.shape[2]], BF16, name=f"{name}_grouped", tag=f"{name}_grouped", align_bytes=64)
             interleave(copy, grouped[:], raw)
             return grouped
 
@@ -70,41 +70,42 @@ def tile_picked_fpn_none_p_kernel(
             return codes, plane
 
         w2_codes, w2_plane = quantize("w2", group("w2", w2_raw[:], nc.scalar.copy))
-        coarse = pool.tile([P, V + 16], F32, name="coarse", align_bytes=64)
-        nc.vector.memset(coarse[:, V:], 0.0)
-        pieces = [(0, 128, nc.scalar.copy), (128, 256, nc.vector.tensor_copy), (384, 128, nc.scalar.copy)]
-        grouped = [group(f"s{v0}", s_raw[:, :, v0 : v0 + width], copy) for v0, width, copy in pieces]
-        for (v0, width, copy), values in zip(pieces, grouped):
+        coarse = pool.tile([P, 1408], F32, name="coarse", align_bytes=64)
+        nc.gpsimd.memset(coarse[:, V:], 0.0)
+        on_vector, on_scalar = nc.vector.tensor_copy, nc.scalar.copy
+        pieces = [
+            (0, 128, on_vector, on_scalar), (128, 128, on_scalar, on_scalar), (256, 128, on_vector, on_scalar),
+            (384, 64, on_vector, on_vector), (448, 64, on_scalar, on_vector),
+        ]
+        grouped = [group(f"s{v0}", s_raw[:, :, v0 : v0 + width], copy) for v0, width, copy, empty in pieces]
+        for (v0, width, copy, empty), values in zip(pieces, grouped):
             codes, plane = quantize(f"s{v0}", values)
-            acc = psum.tile([P, width], F32, name=f"coarse_acc{v0}")
+            acc = psum.tile([P, width], F32, name=f"coarse_acc{v0}", tag=f"coarse_acc{v0}")
             nc.tensor.matmul_mx(
                 out=acc[:], lhsT=w2_codes[:].bitcast(FP8X4), lhsT_scale=w2_plane[:],
                 rhs=codes[:].bitcast(FP8X4), rhs_scale=plane[:], start=True, stop=True,
             )
-            copy(out=coarse[:, v0 : v0 + width], in_=acc[:])
-
-        w1_codes, w1_plane = quantize("w1", group("w1", w1_raw[:], nc.scalar.copy))
+            empty(out=coarse[:, v0 : v0 + width], in_=acc[:])
 
         for r in range(4):
             nc.sync.dma_start(
                 x_plane[r:P:32, :].bitcast(I32), scale_picked[112 + r : P : 4, :].bitcast(I32)
             )
 
+        def pick_words(h, tag):
+            tile = pool.tile([P, S // 2], U32, name=f"picked{h}", tag=tag, align_bytes=64)
+            nc.vector.tensor_copy(tile[:], word_table[:].bitcast(U32).indirect(offs_sb[:, 32 * h : 32 * (h + 1)]))
+            return tile
+
         parents = pool.tile([P, S], F32, name="parents", align_bytes=64)
-        for q in range(2):
-            nc.vector.tensor_copy(
-                parents[:, 512 * q : 512 * (q + 1)],
-                coarse[:].indirect(par_sb[:, 32 * q : 32 * (q + 1)]),
-            )
+        nc.vector.tensor_copy(parents[:], coarse[:].indirect(par_sb[:]))
+        picked = [pick_words(0, "picked0")]
+        w1_codes, w1_plane = quantize("w1", group("w1", w1_raw[:], nc.scalar.copy))
+        picked.append(pick_words(1, "w1_grouped"))
 
         results = [pool.tile([P, 256], F32, name=f"result{b}", align_bytes=64) for b in range(4)]
-        picked = [pool.tile([P, S // 2], U32, name=f"picked{h}", align_bytes=64) for h in range(2)]
-        for h in range(2):
-            nc.vector.tensor_copy(
-                picked[h][:], word_table[:].bitcast(U32).indirect(offs_sb[:, 32 * h : 32 * (h + 1)])
-            )
-        for j0, step in ((0, 512), (512, 128), (640, 128), (768, 128), (896, 128)):
-            acc = psum.tile([P, step], F32, name=f"fine_acc{j0}")
+        for j0, step, bank in ((0, 512, "fine0"), (512, 128, "fine1"), (640, 128, "fine2"), (768, 128, "coarse_acc128"), (896, 128, "coarse_acc0")):
+            acc = psum.tile([P, step], F32, name=f"fine_acc{j0}", tag=bank)
             nc.tensor.matmul_mx(
                 out=acc[:], lhsT=w1_codes[:].bitcast(FP8X4), lhsT_scale=w1_plane[:],
                 rhs=picked[j0 // 512][:, j0 % 512 : j0 % 512 + step].bitcast(FP8X4),
@@ -116,7 +117,8 @@ def tile_picked_fpn_none_p_kernel(
                 block = j // 256
                 nc.vector.tensor_tensor(
                     results[block][:, j % 256 : j % 256 + width],
-                    acc[:, j - j0 : j - j0 + width], parents[:, j : j + width], ADD,
+                    acc[:, j - j0 : j - j0 + width],
+                    parents[:, j : j + width], ADD,
                 )
                 if (j + width) % 256 == 0:
                     nc.sync.dma_start(out[:, 256 * block : 256 * (block + 1)], results[block][:])

@@ -44,16 +44,18 @@ def tile_picked_fpn_none_p_kernel(
         w2_raw = pool.tile([P, PACK, N], F32, name="w2_raw", align_bytes=64)
         s_raw = pool.tile([P, PACK, V], F32, name="s_raw", align_bytes=64)
 
+        zeros = pool.tile([P, 16], F32, name="zeros", align_bytes=64)
+        nc.vector.memset(zeros[:], 0.0)
         nc.vector.memset(scale_table[0:112, :].bitcast(I32), 0)
         nc.vector.memset(x_plane[:].bitcast(I32), 0)
 
-        nc.sync.dma_start(scale_table[112:P, :].bitcast(I32), x_scales[0].bitcast(I32))
+        nc.scalar.dma_start(scale_table[112:P, :].bitcast(I32), x_scales[0].bitcast(I32))
         nc.sync.dma_start(offs_sb[:], offs)
         nc.sync.dma_start(w2_raw[:], w2.rearrange("(p j) m -> p j m", j=PACK))
         nc.sync.dma_start(s_raw[:], sT.rearrange("(p j) v -> p j v", j=PACK))
+        nc.sync.dma_start(w1_raw[:], w1.rearrange("(p j) m -> p j m", j=PACK))
         nc.sync.dma_start(par_sb[:], par)
         nc.sync.dma_start(word_table[:], x_words[0].rearrange("p c r -> p (c r)").bitcast(I32))
-        nc.sync.dma_start(w1_raw[:], w1.rearrange("(p j) m -> p j m", j=PACK))
 
         nc.vector.tensor_copy(scale_picked[:], scale_table[:].indirect(offs_sb[:]))
 
@@ -69,9 +71,10 @@ def tile_picked_fpn_none_p_kernel(
             nc.vector.quantize_mx(out=codes[:].bitcast(FP8X4), scales=plane[:], in_=grouped[:])
             return codes, plane
 
-        w2_codes, w2_plane = quantize("w2", group("w2", w2_raw[:], nc.scalar.copy))
         coarse = pool.tile([P, 1408], F32, name="coarse", align_bytes=64)
-        nc.gpsimd.memset(coarse[:, V:], 0.0)
+        nc.scalar.copy(out=coarse[:, V : V + 16], in_=zeros[:])
+        nc.gpsimd.memset(coarse[:, V + 16 :], 0.0)
+        w2_codes, w2_plane = quantize("w2", group("w2", w2_raw[:], nc.scalar.copy))
         on_vector, on_scalar = nc.vector.tensor_copy, nc.scalar.copy
         pieces = [
             (0, 128, on_vector, on_scalar), (128, 128, on_scalar, on_scalar), (256, 128, on_vector, on_scalar),
@@ -87,6 +90,8 @@ def tile_picked_fpn_none_p_kernel(
             )
             empty(out=coarse[:, v0 : v0 + width], in_=acc[:])
 
+        w1_codes, w1_plane = quantize("w1", group("w1", w1_raw[:], nc.scalar.copy))
+
         for r in range(4):
             nc.sync.dma_start(
                 x_plane[r:P:32, :].bitcast(I32), scale_picked[112 + r : P : 4, :].bitcast(I32)
@@ -99,9 +104,7 @@ def tile_picked_fpn_none_p_kernel(
 
         parents = pool.tile([P, S], F32, name="parents", align_bytes=64)
         nc.vector.tensor_copy(parents[:], coarse[:].indirect(par_sb[:]))
-        picked = [pick_words(0, "picked0")]
-        w1_codes, w1_plane = quantize("w1", group("w1", w1_raw[:], nc.scalar.copy))
-        picked.append(pick_words(1, "w1_grouped"))
+        picked = [pick_words(h, f"picked{h}") for h in range(2)]
 
         results = [pool.tile([P, 256], F32, name=f"result{b}", align_bytes=64) for b in range(4)]
         for j0, step, bank in ((0, 512, "fine0"), (512, 128, "fine1"), (640, 128, "fine2"), (768, 128, "coarse_acc128"), (896, 128, "coarse_acc0")):

@@ -107,7 +107,7 @@ def tile_picked_fpn_none_p_kernel(
         picked = [pick_words(h, f"picked{h}") for h in range(2)]
 
         results = [pool.tile([P, 256], F32, name=f"result{b}", align_bytes=64) for b in range(4)]
-        for j0, step, bank in ((0, 512, "fine0"), (512, 128, "fine1"), (640, 128, "fine2"), (768, 128, "coarse_acc128"), (896, 128, "coarse_acc0")):
+        for j0, step, bank in ((0, 256, "fine0"), (256, 256, "coarse_acc256"), (512, 128, "fine1"), (640, 128, "fine2"), (768, 128, "coarse_acc128"), (896, 128, "coarse_acc0")):
             acc = psum.tile([P, step], F32, name=f"fine_acc{j0}", tag=bank)
             nc.tensor.matmul_mx(
                 out=acc[:], lhsT=w1_codes[:].bitcast(FP8X4), lhsT_scale=w1_plane[:],

@@ -77,12 +77,12 @@ def tile_picked_fpn_none_p_kernel(
         w2_codes, w2_plane = quantize("w2", group("w2", w2_raw[:], nc.scalar.copy))
         on_vector, on_scalar = nc.vector.tensor_copy, nc.scalar.copy
         pieces = [
-            (0, 128, on_vector, on_scalar), (128, 128, on_scalar, on_scalar), (256, 128, on_vector, on_scalar),
+            (0, 128, on_vector, on_vector), (128, 128, on_scalar, on_vector), (256, 128, on_vector, on_vector),
             (384, 64, on_vector, on_vector), (448, 64, on_scalar, on_vector),
         ]
         grouped = [group(f"s{v0}", s_raw[:, :, v0 : v0 + width], copy) for v0, width, copy, empty in pieces]
-        for (v0, width, copy, empty), values in zip(pieces, grouped):
-            codes, plane = quantize(f"s{v0}", values)
+        quantized = [quantize(f"s{v0}", values) for (v0, width, copy, empty), values in zip(pieces, grouped)]
+        for (v0, width, copy, empty), (codes, plane) in zip(pieces, quantized):
             acc = psum.tile([P, width], F32, name=f"coarse_acc{v0}", tag=f"coarse_acc{v0}")
             nc.tensor.matmul_mx(
                 out=acc[:], lhsT=w2_codes[:].bitcast(FP8X4), lhsT_scale=w2_plane[:],

@@ -13,10 +13,13 @@ U16 = mybir.dt.uint16
 U8 = mybir.dt.uint8
 FP8X4 = mybir.dt.float8_e4m3fn_x4
 ADD = mybir.AluOpType.add
+COPY = mybir.ActivationFunctionType.Copy
 
 P = 128
 PACK = 4
 LIST_ROWS = 16
+BLOCK = 256
+FIRST = 640
 
 
 def interleave(copy, grouped, raw):
@@ -33,34 +36,30 @@ def tile_picked_fpn_none_p_kernel(
     with ExitStack() as ctx:
         pool = ctx.enter_context(tc.tile_pool(name="sbuf", bufs=1))
         psum = ctx.enter_context(tc.psum_pool(name="psum", bufs=1))
+        late = ctx.enter_context(tc.tile_pool(name="late", bufs=1))
 
         offs_sb = pool.tile([P, S // LIST_ROWS], U16, name="offs_sb")
         par_sb = pool.tile([P, S // LIST_ROWS], U16, name="par_sb")
         word_table = pool.tile([P, T], I32, name="word_table", align_bytes=64)
         scale_table = pool.tile([P, T], U8, name="scale_table", align_bytes=64)
-        scale_picked = pool.tile([P, S], U8, name="scale_picked", align_bytes=64)
         x_plane = pool.tile([P, S], U8, name="x_plane", align_bytes=64)
-        w1_raw = pool.tile([P, PACK, N], F32, name="w1_raw", align_bytes=64)
+        w1_raw = late.tile([P, PACK, N], F32, name="w1_raw", align_bytes=64, offset=1280)
         w2_raw = pool.tile([P, PACK, N], F32, name="w2_raw", align_bytes=64)
-        s_raw = pool.tile([P, PACK, V], F32, name="s_raw", align_bytes=64)
+        s_raw = pool.tile([P, PACK, V], F32, name="s_raw", tag="s_raw", align_bytes=64)
 
-        zeros = pool.tile([P, 16], F32, name="zeros", align_bytes=64)
-        nc.vector.memset(zeros[:], 0.0)
-        nc.vector.memset(scale_table[0:112, :].bitcast(I32), 0)
+        nc.vector.memset(scale_table[:].bitcast(I32), 0)
         nc.vector.memset(x_plane[:].bitcast(I32), 0)
 
-        nc.scalar.dma_start(scale_table[112:P, :].bitcast(I32), x_scales[0].bitcast(I32))
-        nc.sync.dma_start(offs_sb[:], offs)
         nc.sync.dma_start(w2_raw[:], w2.rearrange("(p j) m -> p j m", j=PACK))
         nc.sync.dma_start(s_raw[:], sT.rearrange("(p j) v -> p j v", j=PACK))
-        nc.sync.dma_start(w1_raw[:], w1.rearrange("(p j) m -> p j m", j=PACK))
+        nc.sync.dma_start(offs_sb[:], offs)
+        nc.sync.dma_start(scale_table[32:96:4, :].bitcast(I32), x_scales[0].bitcast(I32))
         nc.sync.dma_start(par_sb[:], par)
         nc.sync.dma_start(word_table[:], x_words[0].rearrange("p c r -> p (c r)").bitcast(I32))
-
-        nc.vector.tensor_copy(scale_picked[:], scale_table[:].indirect(offs_sb[:]))
+        nc.sync.dma_start(w1_raw[:], w1.rearrange("(p j) m -> p j m", j=PACK))
 
         def group(name, raw, copy):
-            grouped = pool.tile([P, PACK * raw.shape[2]], BF16, name=f"{name}_grouped", tag=f"{name}_grouped", align_bytes=64)
+            grouped = pool.tile([P, PACK * raw.shape[2]], BF16, name=f"{name}_grouped", align_bytes=64)
             interleave(copy, grouped[:], raw)
             return grouped
 
@@ -71,57 +70,62 @@ def tile_picked_fpn_none_p_kernel(
             nc.vector.quantize_mx(out=codes[:].bitcast(FP8X4), scales=plane[:], in_=grouped[:])
             return codes, plane
 
-        coarse = pool.tile([P, 1408], F32, name="coarse", align_bytes=64)
-        nc.scalar.copy(out=coarse[:, V : V + 16], in_=zeros[:])
-        nc.gpsimd.memset(coarse[:, V + 16 :], 0.0)
-        w2_codes, w2_plane = quantize("w2", group("w2", w2_raw[:], nc.scalar.copy))
-        on_vector, on_scalar = nc.vector.tensor_copy, nc.scalar.copy
-        pieces = [
-            (0, 128, on_vector, on_vector), (128, 128, on_scalar, on_vector), (256, 128, on_vector, on_vector),
-            (384, 64, on_vector, on_vector), (448, 64, on_scalar, on_vector),
-        ]
-        grouped = [group(f"s{v0}", s_raw[:, :, v0 : v0 + width], copy) for v0, width, copy, empty in pieces]
-        quantized = [quantize(f"s{v0}", values) for (v0, width, copy, empty), values in zip(pieces, grouped)]
-        for (v0, width, copy, empty), (codes, plane) in zip(pieces, quantized):
-            acc = psum.tile([P, width], F32, name=f"coarse_acc{v0}", tag=f"coarse_acc{v0}")
+        def product(acc, weights, codes, plane):
             nc.tensor.matmul_mx(
-                out=acc[:], lhsT=w2_codes[:].bitcast(FP8X4), lhsT_scale=w2_plane[:],
-                rhs=codes[:].bitcast(FP8X4), rhs_scale=plane[:], start=True, stop=True,
+                out=acc, lhsT=weights[0][:].bitcast(FP8X4), lhsT_scale=weights[1][:],
+                rhs=codes.bitcast(FP8X4), rhs_scale=plane, start=True, stop=True,
             )
-            empty(out=coarse[:, v0 : v0 + width], in_=acc[:])
 
-        w1_codes, w1_plane = quantize("w1", group("w1", w1_raw[:], nc.scalar.copy))
+        on_vector, on_scalar = nc.vector.tensor_copy, nc.scalar.copy
+        w2_mx = quantize("w2", group("w2", w2_raw[:], on_scalar))
 
+        pieces = [(0, 128, on_vector), (128, 128, on_scalar), (256, 128, on_vector), (384, 128, on_scalar)]
+        grouped = [group(f"s{v0}", s_raw[:, :, v0 : v0 + width], copy) for v0, width, copy in pieces]
+        quantized = [quantize(f"s{v0}", values) for (v0, width, copy), values in zip(pieces, grouped)]
+
+        scale_picked = pool.tile([P, S], U8, name="scale_picked", tag="s_raw", align_bytes=64)
+        nc.vector.tensor_copy(scale_picked[:], scale_table[:].indirect(offs_sb[:]))
         for r in range(4):
             nc.sync.dma_start(
-                x_plane[r:P:32, :].bitcast(I32), scale_picked[112 + r : P : 4, :].bitcast(I32)
+                x_plane[r:P:32, :].bitcast(I32), scale_picked[32 + 4 * r : 96 : 16, :].bitcast(I32)
             )
 
-        def pick_words(h, tag):
-            tile = pool.tile([P, S // 2], U32, name=f"picked{h}", tag=tag, align_bytes=64)
-            nc.vector.tensor_copy(tile[:], word_table[:].bitcast(U32).indirect(offs_sb[:, 32 * h : 32 * (h + 1)]))
-            return tile
+        coarse = pool.tile([P, V], F32, name="coarse", align_bytes=64)
+        for i, ((v0, width, copy), (codes, plane)) in enumerate(zip(pieces, quantized)):
+            acc = psum.tile([P, width], F32, name=f"coarse_acc{v0}", tag=f"bank{7 - i}")
+            product(acc[:], w2_mx, codes[:], plane[:])
+            on_scalar(out=coarse[:, v0 : v0 + width], in_=acc[:])
 
-        parents = pool.tile([P, S], F32, name="parents", align_bytes=64)
-        nc.vector.tensor_copy(parents[:], coarse[:].indirect(par_sb[:]))
-        picked = [pick_words(h, f"picked{h}") for h in range(2)]
+        columns = BLOCK // LIST_ROWS
+        blocks = S // BLOCK
+        parents = [pool.tile([P, BLOCK], F32, name=f"parents{b}", align_bytes=64) for b in range(blocks // 2)]
 
-        results = [pool.tile([P, 256], F32, name=f"result{b}", align_bytes=64) for b in range(4)]
-        for j0, step, bank in ((0, 256, "fine0"), (256, 256, "coarse_acc256"), (512, 128, "fine1"), (640, 128, "fine2"), (768, 128, "coarse_acc128"), (896, 128, "coarse_acc0")):
-            acc = psum.tile([P, step], F32, name=f"fine_acc{j0}", tag=bank)
-            nc.tensor.matmul_mx(
-                out=acc[:], lhsT=w1_codes[:].bitcast(FP8X4), lhsT_scale=w1_plane[:],
-                rhs=picked[j0 // 512][:, j0 % 512 : j0 % 512 + step].bitcast(FP8X4),
-                rhs_scale=x_plane[:, j0 : j0 + step],
-                start=True, stop=True,
-            )
-            for j in range(j0, j0 + step, 256):
-                width = min(step, 256)
-                block = j // 256
-                nc.vector.tensor_tensor(
-                    results[block][:, j % 256 : j % 256 + width],
-                    acc[:, j - j0 : j - j0 + width],
-                    parents[:, j : j + width], ADD,
-                )
-                if (j + width) % 256 == 0:
-                    nc.sync.dma_start(out[:, 256 * block : 256 * (block + 1)], results[block][:])
+        def parent_window(b):
+            return coarse[:].indirect(par_sb[:, columns * b : columns * (b + 1)])
+
+        nc.scalar.activation(parents[0][:], parent_window(0), COPY)
+        nc.scalar.activation(parents[1][:], parent_window(1), COPY)
+
+        def pick_words(tile, j0):
+            rows = offs_sb[:, j0 // LIST_ROWS : (j0 + tile.shape[1]) // LIST_ROWS]
+            nc.vector.tensor_copy(tile[:], word_table[:].bitcast(U32).indirect(rows))
+
+        first = pool.tile([P, FIRST], U32, name="picked_first", align_bytes=64)
+        pick_words(first, 0)
+        w1_mx = quantize("w1", group("w1", w1_raw[:], on_scalar))
+        second = late.tile([P, S - FIRST], U32, name="picked_second", align_bytes=64, offset=0)
+        pick_words(second, FIRST)
+        for b in range(blocks // 2, blocks):
+            parents.append(late.tile([P, BLOCK], F32, name=f"parents{b}", align_bytes=64, offset=1024 * b))
+            nc.scalar.activation(parents[b][:], parent_window(b), COPY)
+
+        results = [pool.tile([P, BLOCK], F32, name=f"result{b}", align_bytes=64) for b in range(blocks)]
+        passes = [(0, 256), (256, 256), (512, 128), (640, 128), (768, 128), (896, 128)]
+        for i, (j0, step) in enumerate(passes):
+            acc = psum.tile([P, step], F32, name=f"fine_acc{j0}", tag=f"bank{i}")
+            words = first[:, j0 : j0 + step] if j0 < FIRST else second[:, j0 - FIRST : j0 - FIRST + step]
+            product(acc[:], w1_mx, words, x_plane[:, j0 : j0 + step])
+            b, j = divmod(j0, BLOCK)
+            nc.vector.tensor_tensor(results[b][:, j : j + step], acc[:], parents[b][:, j : j + step], ADD)
+            if j + step == BLOCK:
+                nc.sync.dma_start(out[:, BLOCK * b : BLOCK * (b + 1)], results[b][:])

@@ -18,8 +18,8 @@ COPY = mybir.ActivationFunctionType.Copy
 P = 128
 PACK = 4
 LIST_ROWS = 16
-BLOCK = 256
 FIRST = 640
+EARLY = 640
 
 
 def interleave(copy, grouped, raw):
@@ -43,7 +43,7 @@ def tile_picked_fpn_none_p_kernel(
         word_table = pool.tile([P, T], I32, name="word_table", align_bytes=64)
         scale_table = pool.tile([P, T], U8, name="scale_table", align_bytes=64)
         x_plane = pool.tile([P, S], U8, name="x_plane", align_bytes=64)
-        w1_raw = late.tile([P, PACK, N], F32, name="w1_raw", align_bytes=64, offset=1280)
+        w1_raw = late.tile([P, PACK, N], F32, name="w1_raw", align_bytes=64, offset=1024)
         w2_raw = pool.tile([P, PACK, N], F32, name="w2_raw", align_bytes=64)
         s_raw = pool.tile([P, PACK, V], F32, name="s_raw", tag="s_raw", align_bytes=64)
 
@@ -96,36 +96,37 @@ def tile_picked_fpn_none_p_kernel(
             product(acc[:], w2_mx, codes[:], plane[:])
             on_scalar(out=coarse[:, v0 : v0 + width], in_=acc[:])
 
-        columns = BLOCK // LIST_ROWS
-        blocks = S // BLOCK
-        parents = [pool.tile([P, BLOCK], F32, name=f"parents{b}", align_bytes=64) for b in range(blocks // 2)]
-
-        def parent_window(b):
-            return coarse[:].indirect(par_sb[:, columns * b : columns * (b + 1)])
-
-        nc.scalar.activation(parents[0][:], parent_window(0), COPY)
-        nc.scalar.activation(parents[1][:], parent_window(1), COPY)
+        def pick_parents(tile, j0, cuts):
+            for lo, hi in zip(cuts, cuts[1:]):
+                rows = par_sb[:, lo // LIST_ROWS : hi // LIST_ROWS]
+                nc.scalar.activation(tile[:, lo - j0 : hi - j0], coarse[:].indirect(rows), COPY)
 
         def pick_words(tile, j0):
             rows = offs_sb[:, j0 // LIST_ROWS : (j0 + tile.shape[1]) // LIST_ROWS]
             nc.vector.tensor_copy(tile[:], word_table[:].bitcast(U32).indirect(rows))
+
+        early_parents = pool.tile([P, EARLY], F32, name="early_parents", align_bytes=64)
+        pick_parents(early_parents, 0, [0, 256, 640])
 
         first = pool.tile([P, FIRST], U32, name="picked_first", align_bytes=64)
         pick_words(first, 0)
         w1_mx = quantize("w1", group("w1", w1_raw[:], on_scalar))
         second = late.tile([P, S - FIRST], U32, name="picked_second", align_bytes=64, offset=0)
         pick_words(second, FIRST)
-        for b in range(blocks // 2, blocks):
-            parents.append(late.tile([P, BLOCK], F32, name=f"parents{b}", align_bytes=64, offset=1024 * b))
-            nc.scalar.activation(parents[b][:], parent_window(b), COPY)
+        late_parents = late.tile([P, S - EARLY], F32, name="late_parents", align_bytes=64, offset=2048)
+        pick_parents(late_parents, EARLY, [640, 1024])
 
-        results = [pool.tile([P, BLOCK], F32, name=f"result{b}", align_bytes=64) for b in range(blocks)]
-        passes = [(0, 256), (256, 256), (512, 128), (640, 128), (768, 128), (896, 128)]
-        for i, (j0, step) in enumerate(passes):
+        stores = [(0, 128), (128, 256), (384, 256), (640, 384)]
+        results = {j0: pool.tile([P, width], F32, name=f"result{j0}", align_bytes=64) for j0, width in stores}
+        adds = [(0, 128), (128, 256), (384, 256), (640, 128), (768, 128), (896, 128)]
+        for i, (j0, step) in enumerate(adds):
             acc = psum.tile([P, step], F32, name=f"fine_acc{j0}", tag=f"bank{i}")
-            words = first[:, j0 : j0 + step] if j0 < FIRST else second[:, j0 - FIRST : j0 - FIRST + step]
-            product(acc[:], w1_mx, words, x_plane[:, j0 : j0 + step])
-            b, j = divmod(j0, BLOCK)
-            nc.vector.tensor_tensor(results[b][:, j : j + step], acc[:], parents[b][:, j : j + step], ADD)
-            if j + step == BLOCK:
-                nc.sync.dma_start(out[:, BLOCK * b : BLOCK * (b + 1)], results[b][:])
+            cuts = [j0, FIRST, j0 + step] if j0 < FIRST < j0 + step else [j0, j0 + step]
+            for lo, hi in zip(cuts, cuts[1:]):
+                words = first[:, lo:hi] if lo < FIRST else second[:, lo - FIRST : hi - FIRST]
+                product(acc[:, lo - j0 : hi - j0], w1_mx, words, x_plane[:, lo:hi])
+            parents = early_parents[:, j0 : j0 + step] if j0 < EARLY else late_parents[:, j0 - EARLY : j0 - EARLY + step]
+            r0, width = [store for store in stores if store[0] <= j0][-1]
+            nc.vector.tensor_tensor(results[r0][:, j0 - r0 : j0 - r0 + step], acc[:], parents, ADD)
+            if j0 + step == r0 + width:
+                nc.sync.dma_start(out[:, r0 : r0 + width], results[r0][:])

@@ -18,7 +18,7 @@ COPY = mybir.ActivationFunctionType.Copy
 P = 128
 PACK = 4
 LIST_ROWS = 16
-FIRST = 640
+FIRST = 704
 EARLY = 640
 
 
@@ -50,8 +50,8 @@ def tile_picked_fpn_none_p_kernel(
         nc.vector.memset(scale_table[:].bitcast(I32), 0)
         nc.vector.memset(x_plane[:].bitcast(I32), 0)
 
-        nc.sync.dma_start(w2_raw[:], w2.rearrange("(p j) m -> p j m", j=PACK))
         nc.sync.dma_start(s_raw[:], sT.rearrange("(p j) v -> p j v", j=PACK))
+        nc.sync.dma_start(w2_raw[:], w2.rearrange("(p j) m -> p j m", j=PACK))
         nc.sync.dma_start(offs_sb[:], offs)
         nc.sync.dma_start(scale_table[32:96:4, :].bitcast(I32), x_scales[0].bitcast(I32))
         nc.sync.dma_start(par_sb[:], par)
@@ -77,10 +77,10 @@ def tile_picked_fpn_none_p_kernel(
             )
 
         on_vector, on_scalar = nc.vector.tensor_copy, nc.scalar.copy
-        w2_mx = quantize("w2", group("w2", w2_raw[:], on_scalar))
 
         pieces = [(0, 128, on_vector), (128, 128, on_scalar), (256, 128, on_vector), (384, 128, on_scalar)]
         grouped = [group(f"s{v0}", s_raw[:, :, v0 : v0 + width], copy) for v0, width, copy in pieces]
+        w2_mx = quantize("w2", group("w2", w2_raw[:], on_vector))
         quantized = [quantize(f"s{v0}", values) for (v0, width, copy), values in zip(pieces, grouped)]
 
         scale_picked = pool.tile([P, S], U8, name="scale_picked", tag="s_raw", align_bytes=64)

@@ -38,14 +38,14 @@ def tile_picked_fpn_none_p_kernel(
         psum = ctx.enter_context(tc.psum_pool(name="psum", bufs=1))
         late = ctx.enter_context(tc.tile_pool(name="late", bufs=1))
 
-        offs_sb = pool.tile([P, S // LIST_ROWS], U16, name="offs_sb")
-        par_sb = pool.tile([P, S // LIST_ROWS], U16, name="par_sb")
-        word_table = pool.tile([P, T], I32, name="word_table", align_bytes=64)
-        scale_table = pool.tile([P, T], U8, name="scale_table", align_bytes=64)
-        x_plane = pool.tile([P, S], U8, name="x_plane", align_bytes=64)
-        w1_raw = late.tile([P, PACK, N], F32, name="w1_raw", align_bytes=64, offset=1024)
-        w2_raw = pool.tile([P, PACK, N], F32, name="w2_raw", align_bytes=64)
-        s_raw = pool.tile([P, PACK, V], F32, name="s_raw", tag="s_raw", align_bytes=64)
+        offs_sb = pool.tile([P, S // LIST_ROWS], U16, name="offs_sb", align_bytes=256)
+        par_sb = pool.tile([P, S // LIST_ROWS], U16, name="par_sb", align_bytes=256)
+        word_table = pool.tile([P, T], I32, name="word_table", align_bytes=256)
+        scale_table = pool.tile([P, T], U8, name="scale_table", align_bytes=256)
+        x_plane = pool.tile([P, S], U8, name="x_plane", align_bytes=256)
+        w1_raw = late.tile([P, PACK, N], F32, name="w1_raw", align_bytes=256, offset=1024)
+        w2_raw = pool.tile([P, PACK, N], F32, name="w2_raw", align_bytes=256)
+        s_raw = pool.tile([P, PACK, V], F32, name="s_raw", tag="s_raw", align_bytes=256)
 
         nc.vector.memset(scale_table[:].bitcast(I32), 0)
         nc.vector.memset(x_plane[:].bitcast(I32), 0)
@@ -83,7 +83,7 @@ def tile_picked_fpn_none_p_kernel(
         w2_mx = quantize("w2", group("w2", w2_raw[:], on_vector))
         quantized = [quantize(f"s{v0}", values) for (v0, width, copy), values in zip(pieces, grouped)]
 
-        scale_picked = pool.tile([P, S], U8, name="scale_picked", tag="s_raw", align_bytes=64)
+        scale_picked = pool.tile([P, S], U8, name="scale_picked", tag="s_raw", align_bytes=256)
         nc.vector.tensor_copy(scale_picked[:], scale_table[:].indirect(offs_sb[:]))
         for r in range(4):
             nc.sync.dma_start(
@@ -117,7 +117,7 @@ def tile_picked_fpn_none_p_kernel(
         pick_parents(late_parents, EARLY, [640, 1024])
 
         stores = [(0, 128), (128, 256), (384, 256), (640, 384)]
-        results = {j0: pool.tile([P, width], F32, name=f"result{j0}", align_bytes=64) for j0, width in stores}
+        results = {j0: pool.tile([P, width], F32, name=f"result{j0}", align_bytes=256) for j0, width in stores}
         adds = [(0, 128), (128, 256), (384, 256), (640, 128), (768, 128), (896, 128)]
         for i, (j0, step) in enumerate(adds):
             acc = psum.tile([P, step], F32, name=f"fine_acc{j0}", tag=f"bank{i}")

@@ -19,7 +19,7 @@ P = 128
 PACK = 4
 LIST_ROWS = 16
 FIRST = 704
-EARLY = 640
+EARLY = 704
 
 
 def interleave(copy, grouped, raw):
@@ -106,7 +106,7 @@ def tile_picked_fpn_none_p_kernel(
             nc.vector.tensor_copy(tile[:], word_table[:].bitcast(U32).indirect(rows))
 
         early_parents = pool.tile([P, EARLY], F32, name="early_parents", align_bytes=64)
-        pick_parents(early_parents, 0, [0, 256, 640])
+        pick_parents(early_parents, 0, [0, 256, EARLY])
 
         first = pool.tile([P, FIRST], U32, name="picked_first", align_bytes=64)
         pick_words(first, 0)
@@ -114,14 +114,14 @@ def tile_picked_fpn_none_p_kernel(
         second = late.tile([P, S - FIRST], U32, name="picked_second", align_bytes=64, offset=0)
         pick_words(second, FIRST)
         late_parents = late.tile([P, S - EARLY], F32, name="late_parents", align_bytes=64, offset=2048)
-        pick_parents(late_parents, EARLY, [640, 1024])
+        pick_parents(late_parents, EARLY, [EARLY, S])
 
-        stores = [(0, 128), (128, 256), (384, 256), (640, 384)]
+        stores = [(0, 128), (128, 256), (384, 320), (704, 320)]
         results = {j0: pool.tile([P, width], F32, name=f"result{j0}", align_bytes=256) for j0, width in stores}
-        adds = [(0, 128), (128, 256), (384, 256), (640, 128), (768, 128), (896, 128)]
+        adds = [(0, 128), (128, 256), (384, 320), (704, 128), (832, 128), (960, 64)]
         for i, (j0, step) in enumerate(adds):
             acc = psum.tile([P, step], F32, name=f"fine_acc{j0}", tag=f"bank{i}")
-            cuts = [j0, FIRST, j0 + step] if j0 < FIRST < j0 + step else [j0, j0 + step]
+            cuts = [j0, j0 + 256, j0 + step] if step > 256 else [j0, j0 + step]
             for lo, hi in zip(cuts, cuts[1:]):
                 words = first[:, lo:hi] if lo < FIRST else second[:, lo - FIRST : hi - FIRST]
                 product(acc[:, lo - j0 : hi - j0], w1_mx, words, x_plane[:, lo:hi])

@@ -118,10 +118,10 @@ def tile_picked_fpn_none_p_kernel(
 
         stores = [(0, 128), (128, 256), (384, 320), (704, 320)]
         results = {j0: pool.tile([P, width], F32, name=f"result{j0}", align_bytes=256) for j0, width in stores}
-        adds = [(0, 128), (128, 256), (384, 320), (704, 128), (832, 128), (960, 64)]
+        adds = [(0, 128), (128, 128), (256, 128), (384, 128), (512, 192), (704, 128), (832, 128), (960, 64)]
         for i, (j0, step) in enumerate(adds):
             acc = psum.tile([P, step], F32, name=f"fine_acc{j0}", tag=f"bank{i}")
-            cuts = [j0, j0 + 256, j0 + step] if step > 256 else [j0, j0 + step]
+            cuts = [j0, j0 + 128, j0 + step] if step > 128 else [j0, j0 + step]
             for lo, hi in zip(cuts, cuts[1:]):
                 words = first[:, lo:hi] if lo < FIRST else second[:, lo - FIRST : hi - FIRST]
                 product(acc[:, lo - j0 : hi - j0], w1_mx, words, x_plane[:, lo:hi])

@@ -47,14 +47,15 @@ def tile_picked_fpn_none_p_kernel(
         w2_raw = pool.tile([P, PACK, N], F32, name="w2_raw", align_bytes=256)
         s_raw = pool.tile([P, PACK, V], F32, name="s_raw", tag="s_raw", align_bytes=256)
 
-        nc.vector.memset(scale_table[:].bitcast(I32), 0)
+        nc.vector.memset(scale_table[:, : T // 2].bitcast(I32), 0)
+        nc.gpsimd.memset(scale_table[:, T // 2 :].bitcast(I32), 0)
         nc.vector.memset(x_plane[:].bitcast(I32), 0)
 
-        nc.sync.dma_start(s_raw[:], sT.rearrange("(p j) v -> p j v", j=PACK))
-        nc.sync.dma_start(w2_raw[:], w2.rearrange("(p j) m -> p j m", j=PACK))
+        nc.scalar.dma_start(s_raw[:], sT.rearrange("(p j) v -> p j v", j=PACK))
+        nc.scalar.dma_start(w2_raw[:], w2.rearrange("(p j) m -> p j m", j=PACK))
         nc.sync.dma_start(offs_sb[:], offs)
-        nc.sync.dma_start(scale_table[32:96:4, :].bitcast(I32), x_scales[0].bitcast(I32))
         nc.sync.dma_start(par_sb[:], par)
+        nc.sync.dma_start(scale_table[32:96:4, :].bitcast(I32), x_scales[0].bitcast(I32))
         nc.sync.dma_start(word_table[:], x_words[0].rearrange("p c r -> p (c r)").bitcast(I32))
         nc.sync.dma_start(w1_raw[:], w1.rearrange("(p j) m -> p j m", j=PACK))
 

@@ -19,7 +19,8 @@ P = 128
 PACK = 4
 LIST_ROWS = 16
 FIRST = 704
-EARLY = 704
+EARLY = 1024
+SPARE = 16
 
 
 def interleave(copy, grouped, raw):
@@ -91,7 +92,8 @@ def tile_picked_fpn_none_p_kernel(
                 x_plane[r:P:32, :].bitcast(I32), scale_picked[32 + 4 * r : 96 : 16, :].bitcast(I32)
             )
 
-        coarse = pool.tile([P, V], F32, name="coarse", align_bytes=64)
+        coarse = pool.tile([P, V + SPARE], F32, name="coarse", align_bytes=64)
+        nc.gpsimd.memset(coarse[:, V:], 0.0)
         for i, ((v0, width, copy), (codes, plane)) in enumerate(zip(pieces, quantized)):
             acc = psum.tile([P, width], F32, name=f"coarse_acc{v0}", tag=f"bank{7 - i}")
             product(acc[:], w2_mx, codes[:], plane[:])
@@ -107,15 +109,13 @@ def tile_picked_fpn_none_p_kernel(
             nc.vector.tensor_copy(tile[:], word_table[:].bitcast(U32).indirect(rows))
 
         early_parents = pool.tile([P, EARLY], F32, name="early_parents", align_bytes=64)
-        pick_parents(early_parents, 0, [0, 256, EARLY])
+        pick_parents(early_parents, 0, [0, V, EARLY])
 
         first = pool.tile([P, FIRST], U32, name="picked_first", align_bytes=64)
         pick_words(first, 0)
         w1_mx = quantize("w1", group("w1", w1_raw[:], on_scalar))
         second = late.tile([P, S - FIRST], U32, name="picked_second", align_bytes=64, offset=0)
         pick_words(second, FIRST)
-        late_parents = late.tile([P, S - EARLY], F32, name="late_parents", align_bytes=64, offset=2048)
-        pick_parents(late_parents, EARLY, [EARLY, S])
 
         stores = [(0, 128), (128, 256), (384, 320), (704, 320)]
         results = {j0: pool.tile([P, width], F32, name=f"result{j0}", align_bytes=256) for j0, width in stores}
@@ -126,7 +126,7 @@ def tile_picked_fpn_none_p_kernel(
             for lo, hi in zip(cuts, cuts[1:]):
                 words = first[:, lo:hi] if lo < FIRST else second[:, lo - FIRST : hi - FIRST]
                 product(acc[:, lo - j0 : hi - j0], w1_mx, words, x_plane[:, lo:hi])
-            parents = early_parents[:, j0 : j0 + step] if j0 < EARLY else late_parents[:, j0 - EARLY : j0 - EARLY + step]
+            parents = early_parents[:, j0 : j0 + step]
             r0, width = [store for store in stores if store[0] <= j0][-1]
             nc.vector.tensor_tensor(results[r0][:, j0 - r0 : j0 - r0 + step], acc[:], parents, ADD)
             if j0 + step == r0 + width:

from contextlib import ExitStack

import concourse.mybir as mybir

K, T, S, V, N = 512, 4096, 1024, 512, 128
FLOPS = 2 * K * N * (S + V)

F32 = mybir.dt.float32
BF16 = mybir.dt.bfloat16
I32 = mybir.dt.int32
U32 = mybir.dt.uint32
U16 = mybir.dt.uint16
U8 = mybir.dt.uint8
FP8X4 = mybir.dt.float8_e4m3fn_x4
ADD = mybir.AluOpType.add
COPY = mybir.ActivationFunctionType.Copy

P = 128
PACK = 4
LIST_ROWS = 16
FIRST = 704
EARLY = 1024
SPARE = 16


def interleave(copy, grouped, raw):
    copy(
        out=grouped.rearrange("p (c i t) -> p c t i", i=4, t=PACK),
        in_=raw.rearrange("p t (c i) -> p c t i", i=4),
    )


def tile_picked_fpn_none_p_kernel(
    tc, x_words, x_scales, sT, w1, w2, offs, par, out
):
    nc = tc.nc
    with ExitStack() as ctx:
        pool = ctx.enter_context(tc.tile_pool(name="sbuf", bufs=1))
        psum = ctx.enter_context(tc.psum_pool(name="psum", bufs=1))
        late = ctx.enter_context(tc.tile_pool(name="late", bufs=1))

        offs_sb = pool.tile([P, S // LIST_ROWS], U16, name="offs_sb", align_bytes=256)
        par_sb = pool.tile([P, S // LIST_ROWS], U16, name="par_sb", align_bytes=256)
        word_table = pool.tile([P, T], I32, name="word_table", align_bytes=256)
        scale_table = pool.tile([P, T], U8, name="scale_table", align_bytes=256)
        x_plane = pool.tile([P, S], U8, name="x_plane", align_bytes=256)
        w1_raw = late.tile([P, PACK, N], F32, name="w1_raw", align_bytes=256, offset=1024)
        w2_raw = pool.tile([P, PACK, N], F32, name="w2_raw", align_bytes=256)
        s_raw = pool.tile([P, PACK, V], F32, name="s_raw", tag="s_raw", align_bytes=256)

        nc.vector.memset(scale_table[:, : T // 2].bitcast(I32), 0)
        nc.gpsimd.memset(scale_table[:, T // 2 :].bitcast(I32), 0)
        nc.vector.memset(x_plane[:].bitcast(I32), 0)

        nc.scalar.dma_start(s_raw[:], sT.rearrange("(p j) v -> p j v", j=PACK))
        nc.scalar.dma_start(w2_raw[:], w2.rearrange("(p j) m -> p j m", j=PACK))
        nc.sync.dma_start(offs_sb[:], offs)
        nc.sync.dma_start(par_sb[:], par)
        nc.sync.dma_start(scale_table[32:96:4, :].bitcast(I32), x_scales[0].bitcast(I32))
        nc.sync.dma_start(word_table[:], x_words[0].rearrange("p c r -> p (c r)").bitcast(I32))
        nc.sync.dma_start(w1_raw[:], w1.rearrange("(p j) m -> p j m", j=PACK))

        def group(name, raw, copy):
            grouped = pool.tile([P, PACK * raw.shape[2]], BF16, name=f"{name}_grouped", align_bytes=64)
            interleave(copy, grouped[:], raw)
            return grouped

        def quantize(name, grouped):
            width = grouped.shape[1] // PACK
            codes = pool.tile([P, width], U32, name=f"{name}_codes", align_bytes=64)
            plane = pool.tile([P, width], U8, name=f"{name}_plane", align_bytes=64)
            nc.vector.quantize_mx(out=codes[:].bitcast(FP8X4), scales=plane[:], in_=grouped[:])
            return codes, plane

        def product(acc, weights, codes, plane):
            nc.tensor.matmul_mx(
                out=acc, lhsT=weights[0][:].bitcast(FP8X4), lhsT_scale=weights[1][:],
                rhs=codes.bitcast(FP8X4), rhs_scale=plane, start=True, stop=True,
            )

        on_vector, on_scalar = nc.vector.tensor_copy, nc.scalar.copy

        pieces = [(0, 128, on_vector), (128, 128, on_scalar), (256, 128, on_vector), (384, 128, on_scalar)]
        grouped = [group(f"s{v0}", s_raw[:, :, v0 : v0 + width], copy) for v0, width, copy in pieces]
        w2_mx = quantize("w2", group("w2", w2_raw[:], on_vector))
        quantized = [quantize(f"s{v0}", values) for (v0, width, copy), values in zip(pieces, grouped)]

        scale_picked = pool.tile([P, S], U8, name="scale_picked", tag="s_raw", align_bytes=256)
        nc.vector.tensor_copy(scale_picked[:], scale_table[:].indirect(offs_sb[:]))
        for r in range(4):
            nc.sync.dma_start(
                x_plane[r:P:32, :].bitcast(I32), scale_picked[32 + 4 * r : 96 : 16, :].bitcast(I32)
            )

        coarse = pool.tile([P, V + SPARE], F32, name="coarse", align_bytes=64)
        nc.gpsimd.memset(coarse[:, V:], 0.0)
        for i, ((v0, width, copy), (codes, plane)) in enumerate(zip(pieces, quantized)):
            acc = psum.tile([P, width], F32, name=f"coarse_acc{v0}", tag=f"bank{7 - i}")
            product(acc[:], w2_mx, codes[:], plane[:])
            on_scalar(out=coarse[:, v0 : v0 + width], in_=acc[:])

        def pick_parents(tile, j0, cuts):
            for lo, hi in zip(cuts, cuts[1:]):
                rows = par_sb[:, lo // LIST_ROWS : hi // LIST_ROWS]
                nc.scalar.activation(tile[:, lo - j0 : hi - j0], coarse[:].indirect(rows), COPY)

        def pick_words(tile, j0):
            rows = offs_sb[:, j0 // LIST_ROWS : (j0 + tile.shape[1]) // LIST_ROWS]
            nc.vector.tensor_copy(tile[:], word_table[:].bitcast(U32).indirect(rows))

        early_parents = pool.tile([P, EARLY], F32, name="early_parents", align_bytes=64)
        pick_parents(early_parents, 0, [0, V, EARLY])

        first = pool.tile([P, FIRST], U32, name="picked_first", align_bytes=64)
        pick_words(first, 0)
        w1_mx = quantize("w1", group("w1", w1_raw[:], on_scalar))
        second = late.tile([P, S - FIRST], U32, name="picked_second", align_bytes=64, offset=0)
        pick_words(second, FIRST)

        stores = [(0, 128), (128, 256), (384, 320), (704, 320)]
        results = {j0: pool.tile([P, width], F32, name=f"result{j0}", align_bytes=256) for j0, width in stores}
        adds = [(0, 128), (128, 128), (256, 128), (384, 128), (512, 192), (704, 128), (832, 128), (960, 64)]
        for i, (j0, step) in enumerate(adds):
            acc = psum.tile([P, step], F32, name=f"fine_acc{j0}", tag=f"bank{i}")
            cuts = [j0, j0 + 128, j0 + step] if step > 128 else [j0, j0 + step]
            for lo, hi in zip(cuts, cuts[1:]):
                words = first[:, lo:hi] if lo < FIRST else second[:, lo - FIRST : hi - FIRST]
                product(acc[:, lo - j0 : hi - j0], w1_mx, words, x_plane[:, lo:hi])
            parents = early_parents[:, j0 : j0 + step]
            r0, width = [store for store in stores if store[0] <= j0][-1]
            nc.vector.tensor_tensor(results[r0][:, j0 - r0 : j0 - r0 + step], acc[:], parents, ADD)
            if j0 + step == r0 + width:
                nc.sync.dma_start(out[:, r0 : r0 + width], results[r0][:])
